import numpy as np
import ml_dtypes


def mxq(x, axis, fmt="e4m3"):
    dtype, down = {"e4m3": (ml_dtypes.float8_e4m3fn, 7), "e5m2": (ml_dtypes.float8_e5m2, 14)}[fmt]
    v = np.moveaxis(np.asarray(x, np.float32).astype(ml_dtypes.bfloat16).astype(np.float64), axis, -1)
    blocks = v.reshape(v.shape[:-1] + (-1, 32))
    amax = np.abs(blocks).max(-1, keepdims=True)
    byte = np.maximum(np.where(amax > 0, np.frexp(amax)[1] - 1 + 127, 0) - down, 1)
    scale = np.exp2(byte - 127.0)
    codes = (blocks / scale).astype(np.float32).astype(dtype).astype(np.float64)
    return np.moveaxis((codes * scale).reshape(v.shape), -1, axis)


WIDE = False


def mx_kscale(k):
    if not WIDE:
        return np.ones(k)
    levels = np.array([10, -10, 5, -5, 0])
    if k % 512:
        return np.exp2(np.random.permutation(np.resize(levels, k // 32))).repeat(32)
    a = np.empty((k // 512, 16))
    for p in range(k // 512):
        a[p, :8] = np.random.permutation(np.resize(levels, 8))
        for g in range(8):
            far = levels[np.abs(levels - a[p, g]) >= 10]
            a[p, g + 8] = far[np.random.randint(len(far))]
    return np.exp2(a.ravel()).repeat(32)


def f64(x):
    return np.asarray(x).astype(np.float64)


def striped(idx):
    return np.tile(idx.reshape(-1, 16).T, (8, 1)).astype(np.uint16)


def unstriped(offs):
    return offs[:16].T.reshape(-1).astype(np.int64)


E2M1 = np.array([0.0, 0.5, 1.0, 1.5, 2.0, 3.0, 4.0, 6.0, -0.0, -0.5, -1.0, -1.5, -2.0, -3.0, -4.0, -6.0])


def pack_weight(w, fmt):
    k, n = w.shape
    w = f64(np.asarray(w, np.float32).astype(ml_dtypes.bfloat16)).reshape(k // 32, 32, n)
    amax = np.abs(w).max(1)
    if fmt == "e4m3":
        byte = np.frexp(amax)[1] - 1 + 127 - 7
    else:
        mant, ex = np.frexp(amax / 6.0)
        byte = np.where(mant > 0.5, ex, ex - 1) + 127
    byte = np.clip(np.where(amax > 0, byte, 1), 1, 254)
    scaled = (w * np.exp2(127.0 - byte)[:, None, :]).reshape(k, n).astype(np.float32)
    by_word = np.ascontiguousarray(scaled.reshape(k // 512, 128, 4, n).transpose(0, 1, 3, 2))
    if fmt == "e4m3":
        words = by_word.astype(ml_dtypes.float8_e4m3fn).view(np.uint8)
    else:
        c = by_word.astype(ml_dtypes.float4_e2m1fn).view(np.uint8) & 0xF
        words = (c[..., 0::2] | (c[..., 1::2] << 4)).reshape(k // 512, 128, 2 * n)
    return np.ascontiguousarray(words), np.ascontiguousarray(byte.astype(np.uint8).reshape(k // 512, 16, n))


def unpack_weight(words, scales, fmt):
    g, _, n = scales.shape
    words = np.ascontiguousarray(words).reshape(g, 128, n, -1)
    if fmt == "e4m3":
        vals = words.view(ml_dtypes.float8_e4m3fn).astype(np.float64)
    else:
        nib = np.empty((g, 128, n, 4), np.uint8)
        nib[..., 0::2] = words & 0xF
        nib[..., 1::2] = words >> 4
        vals = E2M1[nib]
    vals = vals * np.repeat(np.exp2(scales.astype(np.float64) - 127.0), 8, axis=1)[..., None]
    return vals.transpose(0, 1, 3, 2).reshape(g * 512, n)


def gelu(v):
    return 0.5 * v * (1.0 + np.tanh(np.sqrt(2.0 / np.pi) * (v + 0.044715 * v**3)))


K, H, N, T, S, P = 512, 1536, 512, 4096, 1024, 512

def setup_inputs():
    n = np.random.standard_normal
    s = mx_kscale(K)[:, None]
    u = mx_kscale(H)[:, None]
    tab_words, tab_scales = pack_weight(n((K, T)) * s, "e4m3")
    w2_words, w2_scales = pack_weight(0.7 * n((K, H)) / np.sqrt(K) / s, "e2m1")
    wb_words, wb_scales = pack_weight(n((H, N)) / np.sqrt(H) / u, "e4m3")
    return {
        "tab_words": tab_words, "tab_scales": tab_scales,
        "offs": striped(np.random.permutation(T)[:S]),
        "pos1": striped(np.random.permutation(S)[:P]),
        "pos2": striped(np.random.permutation(S)[:P]),
        "w1": (1.3 * n((K, H)) / np.sqrt(K) / s).astype(np.float32),
        "b1": (0.6 * n(H)).astype(np.float32),
        "w2_words": w2_words, "w2_scales": w2_scales,
        "gain": (np.exp(0.4 * n(H)) * u[:, 0]).astype(np.float32),
        "reading": np.exp(0.5 * n((H, P))).astype(np.float32),
        "wa": (n((H, N)) / np.sqrt(H) / u).astype(np.float32),
        "wb_words": wb_words, "wb_scales": wb_scales,
    }

def reference(tab_words, tab_scales, offs, pos1, pos2, w1, b1, w2_words, w2_scales, gain, reading, wa, wb_words, wb_scales):
    v = unpack_weight(tab_words, tab_scales, "e4m3")[:, unstriped(offs)]
    w2 = unpack_weight(w2_words, w2_scales, "e2m1")
    wb = unpack_weight(wb_words, wb_scales, "e4m3")
    bent = np.tanh((mxq(f64(w1), 0, "e4m3").T @ v) + f64(b1)[:, None])
    h = (bent + (w2.T @ v)) * f64(gain)[:, None]
    xa = h[:, unstriped(pos1)] * f64(reading)
    xb = np.abs(h[:, unstriped(pos2)])
    ya = mxq(f64(wa), 0, "e4m3").T @ mxq(xa, 0, "e4m3")
    yb = wb.T @ mxq(xb, 0, "e4m3")
    return ya * yb

@@ -1,0 +1,288 @@
+from contextlib import ExitStack
+
+import concourse.mybir as mybir
+
+K, H, N, T, S, J = 512, 1536, 512, 4096, 1024, 512
+FLOPS = 2 * (2 * K * H * S + 2 * H * N * J)
+
+F32 = mybir.dt.float32
+BF16 = mybir.dt.bfloat16
+I32 = mybir.dt.int32
+U32 = mybir.dt.uint32
+U16 = mybir.dt.uint16
+U8 = mybir.dt.uint8
+E4M3 = mybir.dt.float8_e4m3fn_x4
+E2M1 = mybir.dt.float4_e2m1fn_x4
+ACT = mybir.ActivationFunctionType
+ALU = mybir.AluOpType
+
+P = 128
+PACK = 4
+PASS = P * PACK
+PASSES = H // PASS
+BANK = 512
+H_TILES = 8
+PIECES = ((0, 256, 0), (256, 128, 2), (384, 128, 3))
+
+
+def tile_list_mitosis_reading_scores_kernel(
+    tc, tab_words, tab_scales, offs, pos1, pos2, w1, b1, w2_words, w2_scales, gain, reading, wa,
+    wb_words, wb_scales, out,
+):
+    nc = tc.nc
+    with ExitStack() as ctx:
+        keep = ctx.enter_context(tc.tile_pool(name="keep", bufs=1))
+        psum = ctx.enter_context(tc.psum_pool(name="psum", bufs=1))
+
+        def sb(name, shape, dtype):
+            return keep.tile(shape, dtype, name=name, align_bytes=64)
+
+        offs_t = sb("offs_t", [P, S // 16], U16)
+        pos1_t = sb("pos1_t", [P, J // 16], U16)
+        pos2_t = sb("pos2_t", [P, J // 16], U16)
+        tabw = sb("tabw", [P, T], U32)
+        tabs = sb("tabs", [P, T], U8)
+        vw = [sb(f"vw{i}", [P, BANK], U32) for i in range(2)]
+        vs = [sb(f"vs{i}", [P, BANK], U8) for i in range(2)]
+        w2w_raw = sb("w2w_raw", [P, 2 * H], U8)
+        w2s_raw = sb("w2s_raw", [P, H], U8)
+        w2w = sb("w2w", [P, 2 * H], U8)
+        w2s = [sb(f"w2s{b}", [P, PASS], U8) for b in range(PASSES)]
+        wbw = sb("wbw", [P, PASSES * N], U32)
+        wbs = sb("wbs", [P, PASSES * N], U8)
+        b1_t = sb("b1_t", [P, PASSES, PACK], F32)
+        gain_t = sb("gain_t", [P, PASSES, PACK], F32)
+        gain_wide = [sb(f"gain_wide{b}", [P, PACK, J], F32) for b in range(PASSES)]
+        rd = [sb(f"rd{b}", [P, PACK, J], F32) for b in range(PASSES)]
+        raw = [sb(f"raw{i}", [P, PACK, BANK], F32) for i in range(4)]
+        wgrp = [sb(f"wgrp{i}", [P, PACK * BANK], BF16) for i in range(2)]
+        xgrp = [sb(f"xgrp{i}", [P, PACK * BANK], BF16) for i in range(2)]
+        h = [sb(f"h{i}", [P, S], F32) for i in range(H_TILES)]
+        xa = [sb(f"xa{i}", [P, PACK, J], F32) for i in range(2)]
+        xb = [sb(f"xb{i}", [P, PACK, J], F32) for i in range(2)]
+
+        def codes(name):
+            return [(sb(f"{name}w{b}", [P, BANK], U32), sb(f"{name}s{b}", [P, BANK], U8)) for b in range(PASSES)]
+
+        w1q, waq, xaq, xbq = codes("w1q"), codes("waq"), codes("xaq"), codes("xbq")
+        banks = [psum.tile([P, BANK], F32, name=f"bank{i}") for i in range(8)]
+
+        for plane in (tabs, w2s_raw, wbs):
+            nc.vector.memset(plane[:].bitcast(I32), 0)
+
+        def load_rows(dst, src):
+            nc.sync.dma_start(out=dst[:], in_=src.rearrange("(p t) c -> p t c", t=PACK))
+
+        def load_w1(b):
+            load_rows(raw[b], w1[:, b * PASS:(b + 1) * PASS])
+
+        def load_scales(dst, src):
+            for q in range(4):
+                nc.sync.dma_start(out=dst[32 * q:32 * q + 4, :].bitcast(I32), in_=src[4 * q:4 * q + 4, :].bitcast(I32))
+
+        nc.sync.dma_start(offs_t[:], offs)
+        nc.sync.dma_start(pos1_t[:], pos1)
+        nc.sync.dma_start(pos2_t[:], pos2)
+        nc.sync.dma_start(out=gain_t[:], in_=gain.rearrange("(b p t) -> p b t", p=P, t=PACK))
+        nc.sync.dma_start(out=b1_t[:], in_=b1.rearrange("(b p t) -> p b t", p=P, t=PACK))
+        nc.sync.dma_start(out=w2w_raw[:].bitcast(I32), in_=w2_words[0].bitcast(I32))
+        w1_first = w1[:, 0:PASS].rearrange("(p t) c -> p t c", t=PACK)
+        for u in range(2):
+            nc.sync.dma_start(out=raw[0][:, 2 * u:2 * u + 2, :], in_=w1_first[:, 2 * u:2 * u + 2, :])
+        load_scales(tabs, tab_scales[0])
+        nc.sync.dma_start(out=tabw[:].bitcast(I32), in_=tab_words[0].rearrange("p c i -> p (c i)").bitcast(I32))
+        load_scales(w2s_raw, w2_scales[0])
+        load_rows(rd[0], reading[0:PASS, :])
+        load_w1(1)
+        load_w1(2)
+        load_rows(rd[1], reading[PASS:2 * PASS, :])
+        load_rows(raw[3], wa[0:PASS, :])
+        load_rows(rd[2], reading[2 * PASS:3 * PASS, :])
+        nc.sync.dma_start(
+            out=wbw[:].bitcast(I32).rearrange("p (a c) -> p a c", a=PASSES),
+            in_=wb_words.rearrange("a p c i -> p a (c i)").bitcast(I32),
+        )
+        for q in range(4):
+            nc.sync.dma_start(
+                out=wbs[32 * q:32 * q + 4, :].bitcast(I32).rearrange("r (a c) -> r a c", a=PASSES),
+                in_=wb_scales[:, 4 * q:4 * q + 4, :].rearrange("a r c -> r a c").bitcast(I32),
+            )
+
+        def quantise(q, grp):
+            nc.vector.quantize_mx(out=q[0][:].bitcast(E4M3), scales=q[1][:], in_=grp[:])
+
+        def w1_views(b):
+            dst = wgrp[b % 2][:].rearrange("p (t m j) -> p m j t", t=PACK, j=PACK)
+            src = raw[b][:].rearrange("p j (m t) -> p m j t", t=PACK)
+            return dst, src
+
+        def woven(grp, src):
+            return (
+                grp[:].rearrange("p (c i t) -> p c t i", i=4, t=PACK),
+                src[:].rearrange("p t (c i) -> p c t i", i=4),
+            )
+
+        nc.vector.tensor_copy(
+            w2w[:].bitcast(U16).rearrange("p (b t m) -> p b m t", t=PACK, m=P),
+            w2w_raw[:].bitcast(U16).rearrange("p (b m t) -> p b m t", t=PACK, m=P),
+        )
+        dst, src = w1_views(0)
+        nc.vector.tensor_copy(dst, src)
+        quantise(w1q[0], wgrp[0])
+        for i in range(2):
+            nc.vector.tensor_copy(vs[i][:], tabs[:].indirect(offs_t[:, 32 * i:32 * (i + 1)]))
+
+        def deal_w2_scales(b):
+            cols = slice(PASS * b, PASS * (b + 1))
+            nc.vector.tensor_copy(
+                w2s[b][:].rearrange("p (t m) -> p m t", t=PACK),
+                w2s_raw[:, cols].rearrange("p (m t) -> p m t", t=PACK),
+            )
+
+        nc.vector.tensor_copy(vw[0][:], tabw[:].indirect(offs_t[:, 0:32]))
+        deal_w2_scales(0)
+        nc.vector.tensor_copy(vw[1][:], tabw[:].indirect(offs_t[:, 32:64]))
+        for b in range(PASSES):
+            nc.scalar.copy(gain_wide[b][:], gain_t[:, b, :].unsqueeze(2).to_broadcast([P, PACK, J]))
+
+        def first_stage(b, t):
+            s = PACK * b + t
+            ht = h[s % H_TILES]
+            cols = slice(P * t, P * (t + 1))
+            for i in range(2):
+                bank_a = banks[(2 * s + i) % 4]
+                bank_b = banks[4 + (2 * s + i) % 4]
+                half = ht[:, BANK * i:BANK * (i + 1)]
+                nc.tensor.matmul_mx(
+                    out=bank_a[:], lhsT=w1q[b][0][:, cols].bitcast(E4M3), lhsT_scale=w1q[b][1][:, cols],
+                    rhs=vw[i][:].bitcast(E4M3), rhs_scale=vs[i][:], start=True, stop=True,
+                )
+                nc.tensor.matmul_mx(
+                    out=bank_b[:], lhsT=w2w[:, 2 * P * s:2 * P * (s + 1)].bitcast(E2M1),
+                    lhsT_scale=w2s[b][:, cols],
+                    rhs=vw[i][:].bitcast(E4M3), rhs_scale=vs[i][:], start=True, stop=True,
+                )
+                nc.scalar.activation(half, bank_a[:], ACT.Tanh, bias=b1_t[:, b, t:t + 1])
+                nc.vector.tensor_tensor(half, bank_b[:], half, ALU.add)
+
+        def scale_reading(b):
+            for t in range(PACK):
+                nc.scalar.activation(rd[b][:, t, :], rd[b][:, t, :], ACT.Copy, scale=gain_t[:, b, t:t + 1])
+
+        def staged(tile, j0, w):
+            return tile[:].rearrange("p t c -> p (t c)")[:, PACK * j0:PACK * (j0 + w)].rearrange("p (t c) -> p t c", t=PACK)
+
+        def pick_b(b, t, j0, w):
+            ht = h[(PACK * b + t) % H_TILES]
+            nc.vector.tensor_tensor(
+                staged(xb[b % 2], j0, w)[:, t, :], ht[:].indirect(pos2_t[:, j0 // 16:(j0 + w) // 16]),
+                gain_wide[b][:, t, j0:j0 + w], ALU.mult,
+            )
+
+        def pick_a(b, t, j0, w):
+            ht = h[(PACK * b + t) % H_TILES]
+            nc.vector.tensor_tensor(
+                staged(xa[b % 2], j0, w)[:, t, :], ht[:].indirect(pos1_t[:, j0 // 16:(j0 + w) // 16]),
+                rd[b][:, t, j0:j0 + w], ALU.mult,
+            )
+
+        def pick(b, t):
+            pick_b(b, t, 0, J)
+            pick_a(b, t, 0, J)
+
+        def prepare_w1(b):
+            dst, src = w1_views(b)
+            nc.scalar.copy(dst, src)
+            quantise(w1q[b], wgrp[b % 2])
+
+        def prepare_wa(b):
+            src = raw[(b + 3) % 4]
+            dst, srcv = woven(wgrp[(b + 1) % 2], src)
+            nc.scalar.copy(dst, srcv)
+            quantise(waq[b], wgrp[(b + 1) % 2])
+
+        def prepare_x(b, j0, w):
+            cols = slice(j0, j0 + w)
+            wide = slice(PACK * j0, PACK * (j0 + w))
+            for grp, src, q, func in ((xgrp[0], xb, xbq, ACT.Abs), (xgrp[1], xa, xaq, ACT.Copy)):
+                nc.scalar.activation(
+                    grp[:, wide].rearrange("p (c i t) -> p c t i", i=4, t=PACK),
+                    staged(src[b % 2], j0, w).rearrange("p t (c i) -> p c t i", i=4),
+                    func,
+                )
+                nc.vector.quantize_mx(out=q[b][0][:, cols].bitcast(E4M3), scales=q[b][1][:, cols], in_=grp[:, wide])
+
+        def score_bank(piece, nt):
+            j0, w, first_bank = PIECES[piece]
+            per_bank = BANK // w
+            return first_bank + nt // per_bank, slice(w * (nt % per_bank), w * (nt % per_bank + 1)), nt % per_bank, per_bank
+
+        def second_stage(piece, b):
+            j0, w, first_bank = PIECES[piece]
+            jc = slice(j0, j0 + w)
+            for side in range(2):
+                for nt in range(4):
+                    bank, cols, place, per_bank = score_bank(piece, nt)
+                    if side == 0:
+                        wc = slice(N * b + P * nt, N * b + P * (nt + 1))
+                        lhs, lhs_scale, xq = wbw[:, wc], wbs[:, wc], xbq[b]
+                    else:
+                        wc = slice(P * nt, P * (nt + 1))
+                        lhs, lhs_scale, xq = waq[b][0][:, wc], waq[b][1][:, wc], xaq[b]
+                    nc.tensor.matmul_mx(
+                        out=banks[4 * side + bank][:, cols], lhsT=lhs.bitcast(E4M3), lhsT_scale=lhs_scale,
+                        rhs=xq[0][:, jc].bitcast(E4M3), rhs_scale=xq[1][:, jc],
+                        start=(b == 0 and place == 0), stop=(b == PASSES - 1 and place == per_bank - 1),
+                    )
+
+        def finish(piece):
+            j0, w, first_bank = PIECES[piece]
+            per_bank = BANK // w
+            for k in range(4 // per_bank):
+                bank = first_bank + k
+                nc.scalar.copy(raw[2][:, bank, :], banks[bank][:])
+                nc.vector.tensor_tensor(raw[3][:, bank, :], banks[4 + bank][:], raw[2][:, bank, :], ALU.mult)
+                rows = out[P * per_bank * k:P * per_bank * (k + 1), j0:j0 + w]
+                nc.sync.dma_start(
+                    out=rows.rearrange("(u p) c -> p u c", p=P),
+                    in_=raw[3][:, bank, :].rearrange("p (u c) -> p u c", c=w),
+                )
+
+        for t in range(PACK):
+            first_stage(0, t)
+        scale_reading(0)
+        deal_w2_scales(1)
+        prepare_w1(1)
+        load_rows(raw[0], wa[PASS:2 * PASS, :])
+        for t in range(PACK):
+            first_stage(1, t)
+        deal_w2_scales(2)
+        prepare_w1(2)
+        load_rows(raw[1], wa[2 * PASS:3 * PASS, :])
+        for t in range(PACK):
+            pick(0, t)
+        scale_reading(1)
+        for t in range(PACK):
+            first_stage(2, t)
+        scale_reading(2)
+        for t in range(PACK):
+            pick(1, t)
+        prepare_wa(0)
+        prepare_x(0, 0, J)
+        prepare_wa(1)
+        prepare_wa(2)
+        prepare_x(1, 0, J)
+        last = PASSES - 1
+        for piece in range(len(PIECES)):
+            for b in range(last):
+                second_stage(piece, b)
+        for piece, (j0, w, first_bank) in enumerate(PIECES):
+            for t in range(PACK):
+                pick_b(last, t, j0, w)
+            for t in range(PACK):
+                pick_a(last, t, j0, w)
+            if piece > 0:
+                finish(piece - 1)
+            prepare_x(last, j0, w)
+            second_stage(piece, last)
+        finish(len(PIECES) - 1)

@@ -21,8 +21,8 @@ PACK = 4
 PASS = P * PACK
 PASSES = H // PASS
 BANK = 512
-H_TILES = 8
-PIECES = ((0, 256, 0), (256, 128, 2), (384, 128, 3))
+H_TILES = 12
+PIECES = ((0, 256, 4), (256, 128, 6), (384, 128, 7))
 
 
 def tile_list_mitosis_reading_scores_kernel(
@@ -47,19 +47,19 @@ def tile_list_mitosis_reading_scores_kernel(
         w2w_raw = sb("w2w_raw", [P, 2 * H], U8)
         w2s_raw = sb("w2s_raw", [P, H], U8)
         w2w = sb("w2w", [P, 2 * H], U8)
-        w2s = [sb(f"w2s{b}", [P, PASS], U8) for b in range(PASSES)]
+        w2s = sb("w2s", [P, H], U8)
         wbw = sb("wbw", [P, PASSES * N], U32)
         wbs = sb("wbs", [P, PASSES * N], U8)
         b1_t = sb("b1_t", [P, PASSES, PACK], F32)
         gain_t = sb("gain_t", [P, PASSES, PACK], F32)
-        gain_wide = [sb(f"gain_wide{b}", [P, PACK, J], F32) for b in range(PASSES)]
         rd = [sb(f"rd{b}", [P, PACK, J], F32) for b in range(PASSES)]
         raw = [sb(f"raw{i}", [P, PACK, BANK], F32) for i in range(4)]
         wgrp = [sb(f"wgrp{i}", [P, PACK * BANK], BF16) for i in range(2)]
         xgrp = [sb(f"xgrp{i}", [P, PACK * BANK], BF16) for i in range(2)]
         h = [sb(f"h{i}", [P, S], F32) for i in range(H_TILES)]
-        xa = [sb(f"xa{i}", [P, PACK, J], F32) for i in range(2)]
-        xb = [sb(f"xb{i}", [P, PACK, J], F32) for i in range(2)]
+        xs = [sb(f"xs{i}", [P, PACK, J], F32) for i in range(4)]
+        xb = [xs[b] for b in range(PASSES)]
+        xa = [xs[(PASSES + b) % 4] for b in range(PASSES)]
 
         def codes(name):
             return [(sb(f"{name}w{b}", [P, BANK], U32), sb(f"{name}s{b}", [P, BANK], U8)) for b in range(PASSES)]
@@ -76,9 +76,9 @@ def tile_list_mitosis_reading_scores_kernel(
         def load_w1(b):
             load_rows(raw[b], w1[:, b * PASS:(b + 1) * PASS])
 
-        def load_scales(dst, src):
-            for q in range(4):
-                nc.sync.dma_start(out=dst[32 * q:32 * q + 4, :].bitcast(I32), in_=src[4 * q:4 * q + 4, :].bitcast(I32))
+        def load_scales(queue, dst, src):
+            for r in range(4):
+                queue.dma_start(out=dst[r:P:32, :].bitcast(I32), in_=src[r:16:4, :].bitcast(I32))
 
         nc.sync.dma_start(offs_t[:], offs)
         nc.sync.dma_start(pos1_t[:], pos1)
@@ -88,25 +88,25 @@ def tile_list_mitosis_reading_scores_kernel(
         nc.sync.dma_start(out=w2w_raw[:].bitcast(I32), in_=w2_words[0].bitcast(I32))
         w1_first = w1[:, 0:PASS].rearrange("(p t) c -> p t c", t=PACK)
         for u in range(2):
-            nc.sync.dma_start(out=raw[0][:, 2 * u:2 * u + 2, :], in_=w1_first[:, 2 * u:2 * u + 2, :])
-        load_scales(tabs, tab_scales[0])
+            nc.sync.dma_start(out=raw[0][:, u, :], in_=w1_first[:, u, :])
+        load_scales(nc.sync, tabs, tab_scales[0])
+        for u in range(2, PACK):
+            nc.sync.dma_start(out=raw[0][:, u, :], in_=w1_first[:, u, :])
+        load_scales(nc.sync, w2s_raw, w2_scales[0])
         nc.sync.dma_start(out=tabw[:].bitcast(I32), in_=tab_words[0].rearrange("p c i -> p (c i)").bitcast(I32))
-        load_scales(w2s_raw, w2_scales[0])
-        load_rows(rd[0], reading[0:PASS, :])
         load_w1(1)
         load_w1(2)
-        load_rows(rd[1], reading[PASS:2 * PASS, :])
-        load_rows(raw[3], wa[0:PASS, :])
-        load_rows(rd[2], reading[2 * PASS:3 * PASS, :])
         nc.sync.dma_start(
             out=wbw[:].bitcast(I32).rearrange("p (a c) -> p a c", a=PASSES),
             in_=wb_words.rearrange("a p c i -> p a (c i)").bitcast(I32),
         )
-        for q in range(4):
+        for r in range(4):
             nc.sync.dma_start(
-                out=wbs[32 * q:32 * q + 4, :].bitcast(I32).rearrange("r (a c) -> r a c", a=PASSES),
-                in_=wb_scales[:, 4 * q:4 * q + 4, :].rearrange("a r c -> r a c").bitcast(I32),
+                out=wbs[r:P:32, :].bitcast(I32).rearrange("q (a c) -> q a c", a=PASSES),
+                in_=wb_scales[:, r:16:4, :].rearrange("a q c -> q a c").bitcast(I32),
             )
+        load_rows(raw[3], wa[0:PASS, :])
+        load_rows(rd[0], reading[0:PASS, :])
 
         def quantise(q, grp):
             nc.vector.quantize_mx(out=q[0][:].bitcast(E4M3), scales=q[1][:], in_=grp[:])
@@ -123,27 +123,21 @@ def tile_list_mitosis_reading_scores_kernel(
             )
 
         nc.vector.tensor_copy(
-            w2w[:].bitcast(U16).rearrange("p (b t m) -> p b m t", t=PACK, m=P),
-            w2w_raw[:].bitcast(U16).rearrange("p (b m t) -> p b m t", t=PACK, m=P),
+            w2w[:].bitcast(U16).rearrange("p (b t m) -> p b t m", t=PACK, m=P),
+            w2w_raw[:].bitcast(U16).rearrange("p (b m t) -> p b t m", t=PACK, m=P),
         )
-        dst, src = w1_views(0)
-        nc.vector.tensor_copy(dst, src)
-        quantise(w1q[0], wgrp[0])
         for i in range(2):
             nc.vector.tensor_copy(vs[i][:], tabs[:].indirect(offs_t[:, 32 * i:32 * (i + 1)]))
+        dst, src = w1_views(0)
+        nc.scalar.copy(dst, src)
+        quantise(w1q[0], wgrp[0])
 
-        def deal_w2_scales(b):
-            cols = slice(PASS * b, PASS * (b + 1))
-            nc.vector.tensor_copy(
-                w2s[b][:].rearrange("p (t m) -> p m t", t=PACK),
-                w2s_raw[:, cols].rearrange("p (m t) -> p m t", t=PACK),
-            )
-
-        nc.vector.tensor_copy(vw[0][:], tabw[:].indirect(offs_t[:, 0:32]))
-        deal_w2_scales(0)
-        nc.vector.tensor_copy(vw[1][:], tabw[:].indirect(offs_t[:, 32:64]))
-        for b in range(PASSES):
-            nc.scalar.copy(gain_wide[b][:], gain_t[:, b, :].unsqueeze(2).to_broadcast([P, PACK, J]))
+        nc.vector.tensor_copy(
+            w2s[:].rearrange("p (b t m) -> p b t m", t=PACK, m=P),
+            w2s_raw[:].rearrange("p (b m t) -> p b t m", t=PACK, m=P),
+        )
+        for i in range(2):
+            nc.vector.tensor_copy(vw[i][:], tabw[:].indirect(offs_t[:, 32 * i:32 * (i + 1)]))
 
         def first_stage(b, t):
             s = PACK * b + t
@@ -159,11 +153,12 @@ def tile_list_mitosis_reading_scores_kernel(
                 )
                 nc.tensor.matmul_mx(
                     out=bank_b[:], lhsT=w2w[:, 2 * P * s:2 * P * (s + 1)].bitcast(E2M1),
-                    lhsT_scale=w2s[b][:, cols],
+                    lhsT_scale=w2s[:, P * s:P * (s + 1)],
                     rhs=vw[i][:].bitcast(E4M3), rhs_scale=vs[i][:], start=True, stop=True,
                 )
                 nc.scalar.activation(half, bank_a[:], ACT.Tanh, bias=b1_t[:, b, t:t + 1])
                 nc.vector.tensor_tensor(half, bank_b[:], half, ALU.add)
+                nc.gpsimd.tensor_scalar(half, half, gain_t[:, b, t:t + 1], 0.0, ALU.mult, ALU.add)
 
         def scale_reading(b):
             for t in range(PACK):
@@ -174,15 +169,12 @@ def tile_list_mitosis_reading_scores_kernel(
 
         def pick_b(b, t, j0, w):
             ht = h[(PACK * b + t) % H_TILES]
-            nc.vector.tensor_tensor(
-                staged(xb[b % 2], j0, w)[:, t, :], ht[:].indirect(pos2_t[:, j0 // 16:(j0 + w) // 16]),
-                gain_wide[b][:, t, j0:j0 + w], ALU.mult,
-            )
+            nc.vector.tensor_copy(staged(xb[b], j0, w)[:, t, :], ht[:].indirect(pos2_t[:, j0 // 16:(j0 + w) // 16]))
 
         def pick_a(b, t, j0, w):
             ht = h[(PACK * b + t) % H_TILES]
             nc.vector.tensor_tensor(
-                staged(xa[b % 2], j0, w)[:, t, :], ht[:].indirect(pos1_t[:, j0 // 16:(j0 + w) // 16]),
+                staged(xa[b], j0, w)[:, t, :], ht[:].indirect(pos1_t[:, j0 // 16:(j0 + w) // 16]),
                 rd[b][:, t, j0:j0 + w], ALU.mult,
             )
 
@@ -201,88 +193,78 @@ def tile_list_mitosis_reading_scores_kernel(
             nc.scalar.copy(dst, srcv)
             quantise(waq[b], wgrp[(b + 1) % 2])
 
-        def prepare_x(b, j0, w):
+        def prepare_x(grp, src, q, func, j0, w):
             cols = slice(j0, j0 + w)
             wide = slice(PACK * j0, PACK * (j0 + w))
-            for grp, src, q, func in ((xgrp[0], xb, xbq, ACT.Abs), (xgrp[1], xa, xaq, ACT.Copy)):
-                nc.scalar.activation(
-                    grp[:, wide].rearrange("p (c i t) -> p c t i", i=4, t=PACK),
-                    staged(src[b % 2], j0, w).rearrange("p t (c i) -> p c t i", i=4),
-                    func,
-                )
-                nc.vector.quantize_mx(out=q[b][0][:, cols].bitcast(E4M3), scales=q[b][1][:, cols], in_=grp[:, wide])
+            nc.scalar.activation(
+                grp[:, wide].rearrange("p (c i t) -> p c t i", i=4, t=PACK),
+                staged(src, j0, w).rearrange("p t (c i) -> p c t i", i=4),
+                func,
+            )
+            nc.vector.quantize_mx(out=q[0][:, cols].bitcast(E4M3), scales=q[1][:, cols], in_=grp[:, wide])
 
-        def score_bank(piece, nt):
+        def scores_a(piece, b):
             j0, w, first_bank = PIECES[piece]
             per_bank = BANK // w
-            return first_bank + nt // per_bank, slice(w * (nt % per_bank), w * (nt % per_bank + 1)), nt % per_bank, per_bank
-
-        def second_stage(piece, b):
-            j0, w, first_bank = PIECES[piece]
             jc = slice(j0, j0 + w)
-            for side in range(2):
-                for nt in range(4):
-                    bank, cols, place, per_bank = score_bank(piece, nt)
-                    if side == 0:
-                        wc = slice(N * b + P * nt, N * b + P * (nt + 1))
-                        lhs, lhs_scale, xq = wbw[:, wc], wbs[:, wc], xbq[b]
-                    else:
-                        wc = slice(P * nt, P * (nt + 1))
-                        lhs, lhs_scale, xq = waq[b][0][:, wc], waq[b][1][:, wc], xaq[b]
-                    nc.tensor.matmul_mx(
-                        out=banks[4 * side + bank][:, cols], lhsT=lhs.bitcast(E4M3), lhsT_scale=lhs_scale,
-                        rhs=xq[0][:, jc].bitcast(E4M3), rhs_scale=xq[1][:, jc],
-                        start=(b == 0 and place == 0), stop=(b == PASSES - 1 and place == per_bank - 1),
-                    )
+            for nt in range(4):
+                place = nt % per_bank
+                wc = slice(P * nt, P * (nt + 1))
+                nc.tensor.matmul_mx(
+                    out=banks[first_bank + nt // per_bank][:, w * place:w * (place + 1)],
+                    lhsT=waq[b][0][:, wc].bitcast(E4M3), lhsT_scale=waq[b][1][:, wc],
+                    rhs=xaq[b][0][:, jc].bitcast(E4M3), rhs_scale=xaq[b][1][:, jc],
+                    start=(b == 0 and place == 0), stop=(b == PASSES - 1 and place == per_bank - 1),
+                )
 
         def finish(piece):
             j0, w, first_bank = PIECES[piece]
             per_bank = BANK // w
             for k in range(4 // per_bank):
                 bank = first_bank + k
-                nc.scalar.copy(raw[2][:, bank, :], banks[bank][:])
-                nc.vector.tensor_tensor(raw[3][:, bank, :], banks[4 + bank][:], raw[2][:, bank, :], ALU.mult)
-                rows = out[P * per_bank * k:P * per_bank * (k + 1), j0:j0 + w]
-                nc.sync.dma_start(
-                    out=rows.rearrange("(u p) c -> p u c", p=P),
-                    in_=raw[3][:, bank, :].rearrange("p (u c) -> p u c", c=w),
+                result = raw[3][:, bank - 4, :].rearrange("p (u c) -> p u c", c=w)
+                nc.vector.tensor_tensor(
+                    result, banks[bank][:].rearrange("p (u c) -> p u c", c=w),
+                    raw[2][:, per_bank * k:per_bank * (k + 1), j0:j0 + w], ALU.mult,
                 )
+                rows = out[P * per_bank * k:P * per_bank * (k + 1), j0:j0 + w]
+                nc.sync.dma_start(out=rows.rearrange("(u p) c -> p u c", p=P), in_=result)
 
-        for t in range(PACK):
-            first_stage(0, t)
-        scale_reading(0)
-        deal_w2_scales(1)
-        prepare_w1(1)
-        load_rows(raw[0], wa[PASS:2 * PASS, :])
-        for t in range(PACK):
-            first_stage(1, t)
-        deal_w2_scales(2)
-        prepare_w1(2)
-        load_rows(raw[1], wa[2 * PASS:3 * PASS, :])
-        for t in range(PACK):
-            pick(0, t)
-        scale_reading(1)
-        for t in range(PACK):
-            first_stage(2, t)
-        scale_reading(2)
-        for t in range(PACK):
-            pick(1, t)
-        prepare_wa(0)
-        prepare_x(0, 0, J)
-        prepare_wa(1)
-        prepare_wa(2)
-        prepare_x(1, 0, J)
-        last = PASSES - 1
-        for piece in range(len(PIECES)):
-            for b in range(last):
-                second_stage(piece, b)
-        for piece, (j0, w, first_bank) in enumerate(PIECES):
+        for b in range(PASSES):
+            if b > 0:
+                prepare_w1(b)
             for t in range(PACK):
-                pick_b(last, t, j0, w)
+                first_stage(b, t)
+        for b in range(1, PASSES):
+            load_rows(raw[b - 1], wa[b * PASS:(b + 1) * PASS, :])
+            load_rows(rd[b], reading[b * PASS:(b + 1) * PASS, :])
+        for b in range(PASSES):
+            for t in range(PACK):
+                pick_b(b, t, 0, J)
+            prepare_x(xgrp[b % 2], xb[b], xbq[b], ACT.Abs, 0, J)
+        for b in range(PASSES):
+            for nt in range(4):
+                wc = slice(N * b + P * nt, N * b + P * (nt + 1))
+                nc.tensor.matmul_mx(
+                    out=banks[nt][:], lhsT=wbw[:, wc].bitcast(E4M3), lhsT_scale=wbs[:, wc],
+                    rhs=xbq[b][0][:].bitcast(E4M3), rhs_scale=xbq[b][1][:], start=(b == 0), stop=(b == PASSES - 1),
+                )
+        last = PASSES - 1
+        for b in range(last):
+            for t in range(PACK):
+                pick_a(b, t, 0, J)
+            prepare_wa(b)
+            prepare_x(xgrp[(b + 1) % 2], xa[b], xaq[b], ACT.Copy, 0, J)
+            for piece in range(len(PIECES)):
+                scores_a(piece, b)
+        prepare_wa(last)
+        for nt in range(4):
+            nc.scalar.copy(raw[2][:, nt, :], banks[nt][:])
+        for piece, (j0, w, first_bank) in enumerate(PIECES):
             for t in range(PACK):
                 pick_a(last, t, j0, w)
             if piece > 0:
                 finish(piece - 1)
-            prepare_x(last, j0, w)
-            second_stage(piece, last)
+            prepare_x(xgrp[(last + 1) % 2], xa[last], xaq[last], ACT.Copy, j0, w)
+            scores_a(piece, last)
         finish(len(PIECES) - 1)

@@ -20,8 +20,9 @@ P = 128
 PACK = 4
 PASS = P * PACK
 PASSES = H // PASS
+SLICES = H // P
 BANK = 512
-H_TILES = 12
+TABLE_CUTS = (0, 512, 1024, 2560, 4096)
 PIECES = ((0, 256, 4), (256, 128, 6), (384, 128, 7))
 
 
@@ -47,7 +48,7 @@ def tile_list_mitosis_reading_scores_kernel(
         w2w_raw = sb("w2w_raw", [P, 2 * H], U8)
         w2s_raw = sb("w2s_raw", [P, H], U8)
         w2w = sb("w2w", [P, 2 * H], U8)
-        w2s = sb("w2s", [P, H], U8)
+        w2s = [sb(f"w2s{s}", [P, P], U8) for s in range(8)]
         wbw = sb("wbw", [P, PASSES * N], U32)
         wbs = sb("wbs", [P, PASSES * N], U8)
         b1_t = sb("b1_t", [P, PASSES, PACK], F32)
@@ -55,16 +56,30 @@ def tile_list_mitosis_reading_scores_kernel(
         rd = [sb(f"rd{b}", [P, PACK, J], F32) for b in range(PASSES)]
         raw = [sb(f"raw{i}", [P, PACK, BANK], F32) for i in range(4)]
         wgrp = [sb(f"wgrp{i}", [P, PACK * BANK], BF16) for i in range(2)]
-        xgrp = [sb(f"xgrp{i}", [P, PACK * BANK], BF16) for i in range(2)]
-        h = [sb(f"h{i}", [P, S], F32) for i in range(H_TILES)]
-        xs = [sb(f"xs{i}", [P, PACK, J], F32) for i in range(4)]
-        xb = [xs[b] for b in range(PASSES)]
-        xa = [xs[(PASSES + b) % 4] for b in range(PASSES)]
+        h = [sb(f"h{i}", [P, S], F32) for i in range(SLICES)]
+        pair = sb("pair", [P, 2 * PACK * J], F32)
+        xs = [sb("xs0", [P, PACK * J], F32)[:], pair[:, 0:PACK * J], pair[:, PACK * J:2 * PACK * J], sb("xs3", [P, PACK * J], F32)[:]]
+
+        def as_woven(tile, k):
+            return tile[:, 2 * BANK * k:2 * BANK * (k + 1)].bitcast(BF16)
+
+        def planes(flat):
+            return flat.rearrange("p (t c) -> p t c", t=PACK)
+
+        early = [planes(xs[b][:]) for b in range(PASSES)]
+        early_woven = [as_woven(xs[3], b % 2) for b in range(PASSES)]
+        wa_woven = [wgrp[1][:], wgrp[1][:], wgrp[0][:]]
+        late = [planes(xs[1][:]), planes(xs[2][:])]
+        late_woven = [as_woven(xs[3], 1), as_woven(xs[3], 0)]
+        piece_picked = [planes(xs[1][:, 0:1024]), planes(pair[:, 1792:2304]), planes(xs[1][:, 256:768])]
+        piece_woven = [as_woven(xs[3], 1)[:, PACK * j0:PACK * (j0 + w)] for j0, w, first_bank in PIECES]
+        piece_result = {4: pair[:, 1536:2048], 5: pair[:, 2048:2560], 6: xs[1][:, 256:768], 7: xs[0][:, 0:512]}
 
         def codes(name):
             return [(sb(f"{name}w{b}", [P, BANK], U32), sb(f"{name}s{b}", [P, BANK], U8)) for b in range(PASSES)]
 
         w1q, waq, xaq, xbq = codes("w1q"), codes("waq"), codes("xaq"), codes("xbq")
+        wbq = [(wbw[:, N * b:N * (b + 1)], wbs[:, N * b:N * (b + 1)]) for b in range(PASSES)]
         banks = [psum.tile([P, BANK], F32, name=f"bank{i}") for i in range(8)]
 
         for plane in (tabs, w2s_raw, wbs):
@@ -76,134 +91,127 @@ def tile_list_mitosis_reading_scores_kernel(
         def load_w1(b):
             load_rows(raw[b], w1[:, b * PASS:(b + 1) * PASS])
 
-        def load_scales(queue, dst, src):
-            for r in range(4):
-                queue.dma_start(out=dst[r:P:32, :].bitcast(I32), in_=src[r:16:4, :].bitcast(I32))
+        def load_wa(b):
+            load_rows(raw[(b + 3) % 4], wa[b * PASS:(b + 1) * PASS, :])
 
-        nc.sync.dma_start(offs_t[:], offs)
-        nc.sync.dma_start(pos1_t[:], pos1)
-        nc.sync.dma_start(pos2_t[:], pos2)
-        nc.sync.dma_start(out=gain_t[:], in_=gain.rearrange("(b p t) -> p b t", p=P, t=PACK))
-        nc.sync.dma_start(out=b1_t[:], in_=b1.rearrange("(b p t) -> p b t", p=P, t=PACK))
-        nc.sync.dma_start(out=w2w_raw[:].bitcast(I32), in_=w2_words[0].bitcast(I32))
+        def load_reading(b):
+            load_rows(rd[b], reading[b * PASS:(b + 1) * PASS, :])
+
+        def load_scales(dst, src):
+            for r in range(4):
+                nc.sync.dma_start(out=dst[r:P:32, :].bitcast(I32), in_=src[r:16:4, :].bitcast(I32))
+
+        def load_wb():
+            nc.sync.dma_start(
+                out=wbw[:].bitcast(I32).rearrange("p (a c) -> p a c", a=PASSES),
+                in_=wb_words.rearrange("a p c i -> p a (c i)").bitcast(I32),
+            )
+            for r in range(4):
+                nc.sync.dma_start(
+                    out=wbs[r:P:32, :].bitcast(I32).rearrange("q (a c) -> q a c", a=PASSES),
+                    in_=wb_scales[:, r:16:4, :].rearrange("a q c -> q a c").bitcast(I32),
+                )
+
         w1_first = w1[:, 0:PASS].rearrange("(p t) c -> p t c", t=PACK)
-        for u in range(2):
+        table = tab_words[0].rearrange("p c i -> p (c i)").bitcast(I32)
+
+        def load_table(first, end):
+            for k in range(first, end):
+                cols = slice(TABLE_CUTS[k], TABLE_CUTS[k + 1])
+                nc.sync.dma_start(out=tabw[:, cols].bitcast(I32), in_=table[:, cols])
+
+        nc.sync.dma_start(out=w2w_raw[:].bitcast(I32), in_=w2_words[0].bitcast(I32))
+        nc.sync.dma_start(offs_t[:], offs)
+        for u in range(PACK):
             nc.sync.dma_start(out=raw[0][:, u, :], in_=w1_first[:, u, :])
-        load_scales(nc.sync, tabs, tab_scales[0])
-        for u in range(2, PACK):
-            nc.sync.dma_start(out=raw[0][:, u, :], in_=w1_first[:, u, :])
-        load_scales(nc.sync, w2s_raw, w2_scales[0])
-        nc.sync.dma_start(out=tabw[:].bitcast(I32), in_=tab_words[0].rearrange("p c i -> p (c i)").bitcast(I32))
+        load_table(0, 2)
+        load_scales(tabs, tab_scales[0])
+        load_table(2, 4)
+        nc.sync.dma_start(out=b1_t[:], in_=b1.rearrange("(b p t) -> p b t", p=P, t=PACK))
+        load_scales(w2s_raw, w2_scales[0])
+        nc.sync.dma_start(out=gain_t[:], in_=gain.rearrange("(b p t) -> p b t", p=P, t=PACK))
+        nc.sync.dma_start(pos2_t[:], pos2)
+        nc.sync.dma_start(pos1_t[:], pos1)
+        load_reading(0)
         load_w1(1)
         load_w1(2)
-        nc.sync.dma_start(
-            out=wbw[:].bitcast(I32).rearrange("p (a c) -> p a c", a=PASSES),
-            in_=wb_words.rearrange("a p c i -> p a (c i)").bitcast(I32),
-        )
-        for r in range(4):
-            nc.sync.dma_start(
-                out=wbs[r:P:32, :].bitcast(I32).rearrange("q (a c) -> q a c", a=PASSES),
-                in_=wb_scales[:, r:16:4, :].rearrange("a q c -> q a c").bitcast(I32),
-            )
-        load_rows(raw[3], wa[0:PASS, :])
-        load_rows(rd[0], reading[0:PASS, :])
+        load_wa(0)
 
-        def quantise(q, grp):
-            nc.vector.quantize_mx(out=q[0][:].bitcast(E4M3), scales=q[1][:], in_=grp[:])
+        def quantise(q, grp, j0, w):
+            nc.vector.quantize_mx(out=q[0][:, j0:j0 + w].bitcast(E4M3), scales=q[1][:, j0:j0 + w], in_=grp)
 
         def w1_views(b):
-            dst = wgrp[b % 2][:].rearrange("p (t m j) -> p m j t", t=PACK, j=PACK)
-            src = raw[b][:].rearrange("p j (m t) -> p m j t", t=PACK)
+            dst = wgrp[b % 2][:].rearrange("p (t m j) -> p m t j", t=PACK, j=PACK)
+            src = raw[b][:].rearrange("p j (m t) -> p m t j", t=PACK)
             return dst, src
-
-        def woven(grp, src):
-            return (
-                grp[:].rearrange("p (c i t) -> p c t i", i=4, t=PACK),
-                src[:].rearrange("p t (c i) -> p c t i", i=4),
-            )
 
         nc.vector.tensor_copy(
             w2w[:].bitcast(U16).rearrange("p (b t m) -> p b t m", t=PACK, m=P),
             w2w_raw[:].bitcast(U16).rearrange("p (b m t) -> p b t m", t=PACK, m=P),
         )
+        dst, src = w1_views(0)
+        nc.vector.tensor_copy(dst, src)
+        quantise(w1q[0], wgrp[0][:], 0, PASS)
         for i in range(2):
             nc.vector.tensor_copy(vs[i][:], tabs[:].indirect(offs_t[:, 32 * i:32 * (i + 1)]))
-        dst, src = w1_views(0)
-        nc.scalar.copy(dst, src)
-        quantise(w1q[0], wgrp[0])
-
-        nc.vector.tensor_copy(
-            w2s[:].rearrange("p (b t m) -> p b t m", t=PACK, m=P),
-            w2s_raw[:].rearrange("p (b m t) -> p b t m", t=PACK, m=P),
-        )
         for i in range(2):
             nc.vector.tensor_copy(vw[i][:], tabw[:].indirect(offs_t[:, 32 * i:32 * (i + 1)]))
 
-        def first_stage(b, t):
-            s = PACK * b + t
-            ht = h[s % H_TILES]
+        def deal_w2_scales(s):
+            first = PASS * (s // PACK) + s % PACK
+            nc.gpsimd.tensor_copy(w2s[s % 8][:], w2s_raw[:, first:PASS * (s // PACK + 1):PACK])
+
+        def first_stage(s, i, turn):
+            b, t = divmod(s, PACK)
             cols = slice(P * t, P * (t + 1))
-            for i in range(2):
-                bank_a = banks[(2 * s + i) % 4]
-                bank_b = banks[4 + (2 * s + i) % 4]
-                half = ht[:, BANK * i:BANK * (i + 1)]
-                nc.tensor.matmul_mx(
-                    out=bank_a[:], lhsT=w1q[b][0][:, cols].bitcast(E4M3), lhsT_scale=w1q[b][1][:, cols],
-                    rhs=vw[i][:].bitcast(E4M3), rhs_scale=vs[i][:], start=True, stop=True,
-                )
-                nc.tensor.matmul_mx(
-                    out=bank_b[:], lhsT=w2w[:, 2 * P * s:2 * P * (s + 1)].bitcast(E2M1),
-                    lhsT_scale=w2s[:, P * s:P * (s + 1)],
-                    rhs=vw[i][:].bitcast(E4M3), rhs_scale=vs[i][:], start=True, stop=True,
-                )
-                nc.scalar.activation(half, bank_a[:], ACT.Tanh, bias=b1_t[:, b, t:t + 1])
-                nc.vector.tensor_tensor(half, bank_b[:], half, ALU.add)
-                nc.gpsimd.tensor_scalar(half, half, gain_t[:, b, t:t + 1], 0.0, ALU.mult, ALU.add)
+            bank_a = banks[turn % 4]
+            bank_b = banks[4 + turn % 4]
+            half = h[s][:, BANK * i:BANK * (i + 1)]
+            nc.tensor.matmul_mx(
+                out=bank_a[:], lhsT=w1q[b][0][:, cols].bitcast(E4M3), lhsT_scale=w1q[b][1][:, cols],
+                rhs=vw[i][:].bitcast(E4M3), rhs_scale=vs[i][:], start=True, stop=True,
+            )
+            nc.tensor.matmul_mx(
+                out=bank_b[:], lhsT=w2w[:, 2 * P * s:2 * P * (s + 1)].bitcast(E2M1), lhsT_scale=w2s[s % 8][:],
+                rhs=vw[i][:].bitcast(E4M3), rhs_scale=vs[i][:], start=True, stop=True,
+            )
+            nc.scalar.activation(half, bank_a[:], ACT.Tanh, bias=b1_t[:, b, t:t + 1])
+            nc.vector.tensor_tensor(half, bank_b[:], half, ALU.add)
+            nc.gpsimd.tensor_scalar(half, half, gain_t[:, b, t:t + 1], 0.0, ALU.mult, ALU.add)
 
-        def scale_reading(b):
-            for t in range(PACK):
-                nc.scalar.activation(rd[b][:, t, :], rd[b][:, t, :], ACT.Copy, scale=gain_t[:, b, t:t + 1])
+        def pick_b(dst, s, j0, w):
+            nc.vector.tensor_copy(dst[:, s % PACK, :], h[s][:].indirect(pos2_t[:, j0 // 16:(j0 + w) // 16]))
 
-        def staged(tile, j0, w):
-            return tile[:].rearrange("p t c -> p (t c)")[:, PACK * j0:PACK * (j0 + w)].rearrange("p (t c) -> p t c", t=PACK)
-
-        def pick_b(b, t, j0, w):
-            ht = h[(PACK * b + t) % H_TILES]
-            nc.vector.tensor_copy(staged(xb[b], j0, w)[:, t, :], ht[:].indirect(pos2_t[:, j0 // 16:(j0 + w) // 16]))
-
-        def pick_a(b, t, j0, w):
-            ht = h[(PACK * b + t) % H_TILES]
+        def pick_a(dst, s, j0, w):
             nc.vector.tensor_tensor(
-                staged(xa[b], j0, w)[:, t, :], ht[:].indirect(pos1_t[:, j0 // 16:(j0 + w) // 16]),
-                rd[b][:, t, j0:j0 + w], ALU.mult,
+                dst[:, s % PACK, :], h[s][:].indirect(pos1_t[:, j0 // 16:(j0 + w) // 16]),
+                rd[s // PACK][:, s % PACK, j0:j0 + w], ALU.mult,
             )
 
-        def pick(b, t):
-            pick_b(b, t, 0, J)
-            pick_a(b, t, 0, J)
+        def pick_early(s):
+            pick_b(early[s // PACK], s, 0, J)
 
         def prepare_w1(b):
             dst, src = w1_views(b)
-            nc.scalar.copy(dst, src)
-            quantise(w1q[b], wgrp[b % 2])
+            for m0 in range(0, P, P // 4):
+                nc.scalar.copy(dst[:, m0:m0 + P // 4], src[:, m0:m0 + P // 4])
+            quantise(w1q[b], wgrp[b % 2][:], 0, PASS)
+
+        def weave(grp, src, func, q, j0, w):
+            dst = grp.rearrange("p (c t) -> p c t", t=PACK)
+            picked = src.rearrange("p t c -> p c t")
+            step = min(w, 512) // 1
+            for c0 in range(0, w // 1, step):
+                nc.scalar.activation(dst[:, c0:c0 + step], picked[:, c0:c0 + step], func)
+            quantise(q, grp, j0, w)
 
         def prepare_wa(b):
-            src = raw[(b + 3) % 4]
-            dst, srcv = woven(wgrp[(b + 1) % 2], src)
-            nc.scalar.copy(dst, srcv)
-            quantise(waq[b], wgrp[(b + 1) % 2])
+            weave(wa_woven[b], raw[(b + 3) % 4][:], ACT.Copy, waq[b], 0, N)
 
-        def prepare_x(grp, src, q, func, j0, w):
-            cols = slice(j0, j0 + w)
-            wide = slice(PACK * j0, PACK * (j0 + w))
-            nc.scalar.activation(
-                grp[:, wide].rearrange("p (c i t) -> p c t i", i=4, t=PACK),
-                staged(src, j0, w).rearrange("p t (c i) -> p c t i", i=4),
-                func,
-            )
-            nc.vector.quantize_mx(out=q[0][:, cols].bitcast(E4M3), scales=q[1][:, cols], in_=grp[:, wide])
+        def prepare_early(b):
+            weave(early_woven[b], early[b], ACT.Abs, xbq[b], 0, J)
 
-        def scores_a(piece, b):
+        def scores_late(piece, b):
             j0, w, first_bank = PIECES[piece]
             per_bank = BANK // w
             jc = slice(j0, j0 + w)
@@ -222,7 +230,7 @@ def tile_list_mitosis_reading_scores_kernel(
             per_bank = BANK // w
             for k in range(4 // per_bank):
                 bank = first_bank + k
-                result = raw[3][:, bank - 4, :].rearrange("p (u c) -> p u c", c=w)
+                result = piece_result[bank].rearrange("p (u c) -> p u c", c=w)
                 nc.vector.tensor_tensor(
                     result, banks[bank][:].rearrange("p (u c) -> p u c", c=w),
                     raw[2][:, per_bank * k:per_bank * (k + 1), j0:j0 + w], ALU.mult,
@@ -230,41 +238,59 @@ def tile_list_mitosis_reading_scores_kernel(
                 rows = out[P * per_bank * k:P * per_bank * (k + 1), j0:j0 + w]
                 nc.sync.dma_start(out=rows.rearrange("(u p) c -> p u c", p=P), in_=result)
 
-        for b in range(PASSES):
-            if b > 0:
-                prepare_w1(b)
-            for t in range(PACK):
-                first_stage(b, t)
-        for b in range(1, PASSES):
-            load_rows(raw[b - 1], wa[b * PASS:(b + 1) * PASS, :])
-            load_rows(rd[b], reading[b * PASS:(b + 1) * PASS, :])
-        for b in range(PASSES):
-            for t in range(PACK):
-                pick_b(b, t, 0, J)
-            prepare_x(xgrp[b % 2], xb[b], xbq[b], ACT.Abs, 0, J)
+        def slices(first, end):
+            for s in range(first, end):
+                for i in range(2):
+                    first_stage(s, i, 2 * s + i)
+                if s - 2 + 8 < SLICES:
+                    deal_w2_scales(s - 2 + 8)
+                pick_early(s - 1)
+
+        for s in range(8):
+            deal_w2_scales(s)
+        for turn, (s, i) in enumerate(((0, 0), (1, 0), (0, 1), (1, 1))):
+            first_stage(s, i, turn)
+        pick_early(0)
+        slices(2, 4)
+        prepare_w1(1)
+        load_wa(1)
+        load_reading(1)
+        load_wa(2)
+        load_reading(2)
+        load_wb()
+        slices(4, 8)
+        prepare_w1(2)
+        slices(8, 12)
+        pick_early(11)
+        prepare_early(0)
+        prepare_early(1)
+        prepare_early(2)
+        prepare_wa(0)
+        prepare_wa(2)
+        prepare_wa(1)
         for b in range(PASSES):
             for nt in range(4):
-                wc = slice(N * b + P * nt, N * b + P * (nt + 1))
+                wc = slice(P * nt, P * (nt + 1))
                 nc.tensor.matmul_mx(
-                    out=banks[nt][:], lhsT=wbw[:, wc].bitcast(E4M3), lhsT_scale=wbs[:, wc],
+                    out=banks[nt][:], lhsT=wbq[b][0][:, wc].bitcast(E4M3), lhsT_scale=wbq[b][1][:, wc],
                     rhs=xbq[b][0][:].bitcast(E4M3), rhs_scale=xbq[b][1][:], start=(b == 0), stop=(b == PASSES - 1),
                 )
         last = PASSES - 1
         for b in range(last):
             for t in range(PACK):
-                pick_a(b, t, 0, J)
-            prepare_wa(b)
-            prepare_x(xgrp[(b + 1) % 2], xa[b], xaq[b], ACT.Copy, 0, J)
-            for piece in range(len(PIECES)):
-                scores_a(piece, b)
-        prepare_wa(last)
-        for nt in range(4):
-            nc.scalar.copy(raw[2][:, nt, :], banks[nt][:])
+                pick_a(late[b], PACK * b + t, 0, J)
+            weave(late_woven[b], late[b], ACT.Copy, xaq[b], 0, J)
+            if b == 0:
+                for nt in range(4):
+                    nc.scalar.copy(raw[2][:, nt, :], banks[nt][:])
+            if b == 0:
+                for piece in range(len(PIECES)):
+                    scores_late(piece, b)
         for piece, (j0, w, first_bank) in enumerate(PIECES):
             for t in range(PACK):
-                pick_a(last, t, j0, w)
-            if piece > 0:
-                finish(piece - 1)
-            prepare_x(xgrp[(last + 1) % 2], xa[last], xaq[last], ACT.Copy, j0, w)
-            scores_a(piece, last)
-        finish(len(PIECES) - 1)
+                pick_a(piece_picked[piece], PACK * last + t, j0, w)
+            weave(piece_woven[piece], piece_picked[piece], ACT.Copy, xaq[last], j0, w)
+            for b in range(1, PASSES):
+                scores_late(piece, b)
+        for piece in range(len(PIECES)):
+            finish(piece)

@@ -48,7 +48,7 @@ def tile_list_mitosis_reading_scores_kernel(
         w2w_raw = sb("w2w_raw", [P, 2 * H], U8)
         w2s_raw = sb("w2s_raw", [P, H], U8)
         w2w = sb("w2w", [P, 2 * H], U8)
-        w2s = [sb(f"w2s{s}", [P, P], U8) for s in range(8)]
+        w2s = [sb(f"w2s{b}", [P, PASS], U8) for b in range(PASSES)]
         wbw = sb("wbw", [P, PASSES * N], U32)
         wbs = sb("wbs", [P, PASSES * N], U8)
         b1_t = sb("b1_t", [P, PASSES, PACK], F32)
@@ -127,22 +127,22 @@ def tile_list_mitosis_reading_scores_kernel(
         load_table(0, 2)
         load_scales(tabs, tab_scales[0])
         load_table(2, 4)
-        nc.sync.dma_start(out=b1_t[:], in_=b1.rearrange("(b p t) -> p b t", p=P, t=PACK))
         load_scales(w2s_raw, w2_scales[0])
+        nc.sync.dma_start(out=b1_t[:], in_=b1.rearrange("(b p t) -> p b t", p=P, t=PACK))
         nc.sync.dma_start(out=gain_t[:], in_=gain.rearrange("(b p t) -> p b t", p=P, t=PACK))
         nc.sync.dma_start(pos2_t[:], pos2)
         nc.sync.dma_start(pos1_t[:], pos1)
-        load_reading(0)
         load_w1(1)
         load_w1(2)
         load_wa(0)
+        load_reading(0)
 
         def quantise(q, grp, j0, w):
             nc.vector.quantize_mx(out=q[0][:, j0:j0 + w].bitcast(E4M3), scales=q[1][:, j0:j0 + w], in_=grp)
 
         def w1_views(b):
-            dst = wgrp[b % 2][:].rearrange("p (t m j) -> p m t j", t=PACK, j=PACK)
-            src = raw[b][:].rearrange("p j (m t) -> p m t j", t=PACK)
+            dst = wgrp[b % 2][:].rearrange("p (t m j) -> p m j t", t=PACK, j=PACK)
+            src = raw[b][:].rearrange("p j (m t) -> p m j t", t=PACK)
             return dst, src
 
         nc.vector.tensor_copy(
@@ -154,12 +154,16 @@ def tile_list_mitosis_reading_scores_kernel(
         quantise(w1q[0], wgrp[0][:], 0, PASS)
         for i in range(2):
             nc.vector.tensor_copy(vs[i][:], tabs[:].indirect(offs_t[:, 32 * i:32 * (i + 1)]))
-        for i in range(2):
-            nc.vector.tensor_copy(vw[i][:], tabw[:].indirect(offs_t[:, 32 * i:32 * (i + 1)]))
 
-        def deal_w2_scales(s):
-            first = PASS * (s // PACK) + s % PACK
-            nc.gpsimd.tensor_copy(w2s[s % 8][:], w2s_raw[:, first:PASS * (s // PACK + 1):PACK])
+        def deal_w2_scales(b):
+            nc.vector.tensor_copy(
+                w2s[b][:].rearrange("p (t m) -> p t m", t=PACK),
+                w2s_raw[:, PASS * b:PASS * (b + 1)].rearrange("p (m t) -> p t m", t=PACK),
+            )
+
+        nc.vector.tensor_copy(vw[0][:], tabw[:].indirect(offs_t[:, 0:32]))
+        deal_w2_scales(0)
+        nc.vector.tensor_copy(vw[1][:], tabw[:].indirect(offs_t[:, 32:64]))
 
         def first_stage(s, i, turn):
             b, t = divmod(s, PACK)
@@ -172,7 +176,7 @@ def tile_list_mitosis_reading_scores_kernel(
                 rhs=vw[i][:].bitcast(E4M3), rhs_scale=vs[i][:], start=True, stop=True,
             )
             nc.tensor.matmul_mx(
-                out=bank_b[:], lhsT=w2w[:, 2 * P * s:2 * P * (s + 1)].bitcast(E2M1), lhsT_scale=w2s[s % 8][:],
+                out=bank_b[:], lhsT=w2w[:, 2 * P * s:2 * P * (s + 1)].bitcast(E2M1), lhsT_scale=w2s[b][:, cols],
                 rhs=vw[i][:].bitcast(E4M3), rhs_scale=vs[i][:], start=True, stop=True,
             )
             nc.scalar.activation(half, bank_a[:], ACT.Tanh, bias=b1_t[:, b, t:t + 1])
@@ -193,20 +197,27 @@ def tile_list_mitosis_reading_scores_kernel(
 
         def prepare_w1(b):
             dst, src = w1_views(b)
-            for m0 in range(0, P, P // 4):
-                nc.scalar.copy(dst[:, m0:m0 + P // 4], src[:, m0:m0 + P // 4])
+            for m0 in range(0, P, P // 1):
+                nc.scalar.copy(dst[:, m0:m0 + P // 1], src[:, m0:m0 + P // 1])
             quantise(w1q[b], wgrp[b % 2][:], 0, PASS)
 
         def weave(grp, src, func, q, j0, w):
-            dst = grp.rearrange("p (c t) -> p c t", t=PACK)
-            picked = src.rearrange("p t c -> p c t")
-            step = min(w, 512) // 1
-            for c0 in range(0, w // 1, step):
+            dst = grp.rearrange("p (c i t) -> p c t i", i=4, t=PACK)
+            picked = src.rearrange("p t (c i) -> p c t i", i=4)
+            step = min(w, 512) // 4
+            for c0 in range(0, w // 4, step):
                 nc.scalar.activation(dst[:, c0:c0 + step], picked[:, c0:c0 + step], func)
             quantise(q, grp, j0, w)
 
         def prepare_wa(b):
-            weave(wa_woven[b], raw[(b + 3) % 4][:], ACT.Copy, waq[b], 0, N)
+            if b in (1,):
+                nc.vector.tensor_copy(
+                    wa_woven[b].rearrange("p (c i t) -> p c t i", i=4, t=PACK),
+                    raw[(b + 3) % 4][:].rearrange("p t (c i) -> p c t i", i=4),
+                )
+                quantise(waq[b], wa_woven[b], 0, N)
+            else:
+                weave(wa_woven[b], raw[(b + 3) % 4][:], ACT.Copy, waq[b], 0, N)
 
         def prepare_early(b):
             weave(early_woven[b], early[b], ACT.Abs, xbq[b], 0, J)
@@ -242,14 +253,12 @@ def tile_list_mitosis_reading_scores_kernel(
             for s in range(first, end):
                 for i in range(2):
                     first_stage(s, i, 2 * s + i)
-                if s - 2 + 8 < SLICES:
-                    deal_w2_scales(s - 2 + 8)
                 pick_early(s - 1)
 
-        for s in range(8):
-            deal_w2_scales(s)
         for turn, (s, i) in enumerate(((0, 0), (1, 0), (0, 1), (1, 1))):
             first_stage(s, i, turn)
+        for b in range(1, PASSES):
+            deal_w2_scales(b)
         pick_early(0)
         slices(2, 4)
         prepare_w1(1)

@@ -48,7 +48,7 @@ def tile_list_mitosis_reading_scores_kernel(
         w2w_raw = sb("w2w_raw", [P, 2 * H], U8)
         w2s_raw = sb("w2s_raw", [P, H], U8)
         w2w = sb("w2w", [P, 2 * H], U8)
-        w2s = [sb(f"w2s{b}", [P, PASS], U8) for b in range(PASSES)]
+        w2s = sb("w2s", [P, H], U8)
         wbw = sb("wbw", [P, PASSES * N], U32)
         wbs = sb("wbs", [P, PASSES * N], U8)
         b1_t = sb("b1_t", [P, PASSES, PACK], F32)
@@ -113,25 +113,19 @@ def tile_list_mitosis_reading_scores_kernel(
                 )
 
         w1_first = w1[:, 0:PASS].rearrange("(p t) c -> p t c", t=PACK)
-        table = tab_words[0].rearrange("p c i -> p (c i)").bitcast(I32)
-
-        def load_table(first, end):
-            for k in range(first, end):
-                cols = slice(TABLE_CUTS[k], TABLE_CUTS[k + 1])
-                nc.sync.dma_start(out=tabw[:, cols].bitcast(I32), in_=table[:, cols])
-
-        nc.sync.dma_start(out=w2w_raw[:].bitcast(I32), in_=w2_words[0].bitcast(I32))
         nc.sync.dma_start(offs_t[:], offs)
-        for u in range(PACK):
-            nc.sync.dma_start(out=raw[0][:, u, :], in_=w1_first[:, u, :])
-        load_table(0, 2)
-        load_scales(tabs, tab_scales[0])
-        load_table(2, 4)
-        load_scales(w2s_raw, w2_scales[0])
-        nc.sync.dma_start(out=b1_t[:], in_=b1.rearrange("(b p t) -> p b t", p=P, t=PACK))
-        nc.sync.dma_start(out=gain_t[:], in_=gain.rearrange("(b p t) -> p b t", p=P, t=PACK))
-        nc.sync.dma_start(pos2_t[:], pos2)
         nc.sync.dma_start(pos1_t[:], pos1)
+        nc.sync.dma_start(pos2_t[:], pos2)
+        nc.sync.dma_start(out=gain_t[:], in_=gain.rearrange("(b p t) -> p b t", p=P, t=PACK))
+        nc.sync.dma_start(out=b1_t[:], in_=b1.rearrange("(b p t) -> p b t", p=P, t=PACK))
+        nc.sync.dma_start(out=w2w_raw[:].bitcast(I32), in_=w2_words[0].bitcast(I32))
+        for u in range(2):
+            nc.sync.dma_start(out=raw[0][:, u, :], in_=w1_first[:, u, :])
+        load_scales(tabs, tab_scales[0])
+        for u in range(2, PACK):
+            nc.sync.dma_start(out=raw[0][:, u, :], in_=w1_first[:, u, :])
+        load_scales(w2s_raw, w2_scales[0])
+        nc.sync.dma_start(out=tabw[:].bitcast(I32), in_=tab_words[0].rearrange("p c i -> p (c i)").bitcast(I32))
         load_w1(1)
         load_w1(2)
         load_wa(0)
@@ -149,21 +143,18 @@ def tile_list_mitosis_reading_scores_kernel(
             w2w[:].bitcast(U16).rearrange("p (b t m) -> p b t m", t=PACK, m=P),
             w2w_raw[:].bitcast(U16).rearrange("p (b m t) -> p b t m", t=PACK, m=P),
         )
-        dst, src = w1_views(0)
-        nc.vector.tensor_copy(dst, src)
-        quantise(w1q[0], wgrp[0][:], 0, PASS)
         for i in range(2):
             nc.vector.tensor_copy(vs[i][:], tabs[:].indirect(offs_t[:, 32 * i:32 * (i + 1)]))
+        dst, src = w1_views(0)
+        nc.scalar.copy(dst, src)
+        quantise(w1q[0], wgrp[0][:], 0, PASS)
 
-        def deal_w2_scales(b):
-            nc.vector.tensor_copy(
-                w2s[b][:].rearrange("p (t m) -> p t m", t=PACK),
-                w2s_raw[:, PASS * b:PASS * (b + 1)].rearrange("p (m t) -> p t m", t=PACK),
-            )
-
-        nc.vector.tensor_copy(vw[0][:], tabw[:].indirect(offs_t[:, 0:32]))
-        deal_w2_scales(0)
-        nc.vector.tensor_copy(vw[1][:], tabw[:].indirect(offs_t[:, 32:64]))
+        nc.vector.tensor_copy(
+            w2s[:].rearrange("p (b t m) -> p b t m", t=PACK, m=P),
+            w2s_raw[:].rearrange("p (b m t) -> p b t m", t=PACK, m=P),
+        )
+        for i in range(2):
+            nc.vector.tensor_copy(vw[i][:], tabw[:].indirect(offs_t[:, 32 * i:32 * (i + 1)]))
 
         def first_stage(s, i, turn):
             b, t = divmod(s, PACK)
@@ -176,7 +167,7 @@ def tile_list_mitosis_reading_scores_kernel(
                 rhs=vw[i][:].bitcast(E4M3), rhs_scale=vs[i][:], start=True, stop=True,
             )
             nc.tensor.matmul_mx(
-                out=bank_b[:], lhsT=w2w[:, 2 * P * s:2 * P * (s + 1)].bitcast(E2M1), lhsT_scale=w2s[b][:, cols],
+                out=bank_b[:], lhsT=w2w[:, 2 * P * s:2 * P * (s + 1)].bitcast(E2M1), lhsT_scale=w2s[:, P * s:P * (s + 1)],
                 rhs=vw[i][:].bitcast(E4M3), rhs_scale=vs[i][:], start=True, stop=True,
             )
             nc.scalar.activation(half, bank_a[:], ACT.Tanh, bias=b1_t[:, b, t:t + 1])
@@ -210,14 +201,7 @@ def tile_list_mitosis_reading_scores_kernel(
             quantise(q, grp, j0, w)
 
         def prepare_wa(b):
-            if b in (1,):
-                nc.vector.tensor_copy(
-                    wa_woven[b].rearrange("p (c i t) -> p c t i", i=4, t=PACK),
-                    raw[(b + 3) % 4][:].rearrange("p t (c i) -> p c t i", i=4),
-                )
-                quantise(waq[b], wa_woven[b], 0, N)
-            else:
-                weave(wa_woven[b], raw[(b + 3) % 4][:], ACT.Copy, waq[b], 0, N)
+            weave(wa_woven[b], raw[(b + 3) % 4][:], ACT.Copy, waq[b], 0, N)
 
         def prepare_early(b):
             weave(early_woven[b], early[b], ACT.Abs, xbq[b], 0, J)
@@ -257,8 +241,6 @@ def tile_list_mitosis_reading_scores_kernel(
 
         for turn, (s, i) in enumerate(((0, 0), (1, 0), (0, 1), (1, 1))):
             first_stage(s, i, turn)
-        for b in range(1, PASSES):
-            deal_w2_scales(b)
         pick_early(0)
         slices(2, 4)
         prepare_w1(1)

from contextlib import ExitStack

import concourse.mybir as mybir

K, H, N, T, S, J = 512, 1536, 512, 4096, 1024, 512
FLOPS = 2 * (2 * K * H * S + 2 * H * N * J)

F32 = mybir.dt.float32
BF16 = mybir.dt.bfloat16
I32 = mybir.dt.int32
U32 = mybir.dt.uint32
U16 = mybir.dt.uint16
U8 = mybir.dt.uint8
E4M3 = mybir.dt.float8_e4m3fn_x4
E2M1 = mybir.dt.float4_e2m1fn_x4
ACT = mybir.ActivationFunctionType
ALU = mybir.AluOpType

P = 128
PACK = 4
PASS = P * PACK
PASSES = H // PASS
SLICES = H // P
BANK = 512
TABLE_CUTS = (0, 512, 1024, 2560, 4096)
PIECES = ((0, 256, 4), (256, 128, 6), (384, 128, 7))


def tile_list_mitosis_reading_scores_kernel(
    tc, tab_words, tab_scales, offs, pos1, pos2, w1, b1, w2_words, w2_scales, gain, reading, wa,
    wb_words, wb_scales, out,
):
    nc = tc.nc
    with ExitStack() as ctx:
        keep = ctx.enter_context(tc.tile_pool(name="keep", bufs=1))
        psum = ctx.enter_context(tc.psum_pool(name="psum", bufs=1))

        def sb(name, shape, dtype):
            return keep.tile(shape, dtype, name=name, align_bytes=64)

        offs_t = sb("offs_t", [P, S // 16], U16)
        pos1_t = sb("pos1_t", [P, J // 16], U16)
        pos2_t = sb("pos2_t", [P, J // 16], U16)
        tabw = sb("tabw", [P, T], U32)
        tabs = sb("tabs", [P, T], U8)
        vw = [sb(f"vw{i}", [P, BANK], U32) for i in range(2)]
        vs = [sb(f"vs{i}", [P, BANK], U8) for i in range(2)]
        w2w_raw = sb("w2w_raw", [P, 2 * H], U8)
        w2s_raw = sb("w2s_raw", [P, H], U8)
        w2w = sb("w2w", [P, 2 * H], U8)
        w2s = sb("w2s", [P, H], U8)
        wbw = sb("wbw", [P, PASSES * N], U32)
        wbs = sb("wbs", [P, PASSES * N], U8)
        b1_t = sb("b1_t", [P, PASSES, PACK], F32)
        gain_t = sb("gain_t", [P, PASSES, PACK], F32)
        rd = [sb(f"rd{b}", [P, PACK, J], F32) for b in range(PASSES)]
        raw = [sb(f"raw{i}", [P, PACK, BANK], F32) for i in range(4)]
        wgrp = [sb(f"wgrp{i}", [P, PACK * BANK], BF16) for i in range(2)]
        h = [sb(f"h{i}", [P, S], F32) for i in range(SLICES)]
        pair = sb("pair", [P, 2 * PACK * J], F32)
        xs = [sb("xs0", [P, PACK * J], F32)[:], pair[:, 0:PACK * J], pair[:, PACK * J:2 * PACK * J], sb("xs3", [P, PACK * J], F32)[:]]

        def as_woven(tile, k):
            return tile[:, 2 * BANK * k:2 * BANK * (k + 1)].bitcast(BF16)

        def planes(flat):
            return flat.rearrange("p (t c) -> p t c", t=PACK)

        early = [planes(xs[b][:]) for b in range(PASSES)]
        early_woven = [as_woven(xs[3], b % 2) for b in range(PASSES)]
        wa_woven = [wgrp[1][:], wgrp[1][:], wgrp[0][:]]
        late = [planes(xs[1][:]), planes(xs[2][:])]
        late_woven = [as_woven(xs[3], 1), as_woven(xs[3], 0)]
        piece_picked = [planes(xs[1][:, 0:1024]), planes(pair[:, 1792:2304]), planes(xs[1][:, 256:768])]
        piece_woven = [as_woven(xs[3], 1)[:, PACK * j0:PACK * (j0 + w)] for j0, w, first_bank in PIECES]
        piece_result = {4: pair[:, 1536:2048], 5: pair[:, 2048:2560], 6: xs[1][:, 256:768], 7: xs[0][:, 0:512]}

        def codes(name):
            return [(sb(f"{name}w{b}", [P, BANK], U32), sb(f"{name}s{b}", [P, BANK], U8)) for b in range(PASSES)]

        w1q, waq, xaq, xbq = codes("w1q"), codes("waq"), codes("xaq"), codes("xbq")
        wbq = [(wbw[:, N * b:N * (b + 1)], wbs[:, N * b:N * (b + 1)]) for b in range(PASSES)]
        banks = [psum.tile([P, BANK], F32, name=f"bank{i}") for i in range(8)]

        for plane in (tabs, w2s_raw, wbs):
            nc.vector.memset(plane[:].bitcast(I32), 0)

        def load_rows(dst, src):
            nc.sync.dma_start(out=dst[:], in_=src.rearrange("(p t) c -> p t c", t=PACK))

        def load_w1(b):
            load_rows(raw[b], w1[:, b * PASS:(b + 1) * PASS])

        def load_wa(b):
            load_rows(raw[(b + 3) % 4], wa[b * PASS:(b + 1) * PASS, :])

        def load_reading(b):
            load_rows(rd[b], reading[b * PASS:(b + 1) * PASS, :])

        def load_scales(dst, src):
            for r in range(4):
                nc.sync.dma_start(out=dst[r:P:32, :].bitcast(I32), in_=src[r:16:4, :].bitcast(I32))

        def load_wb():
            nc.sync.dma_start(
                out=wbw[:].bitcast(I32).rearrange("p (a c) -> p a c", a=PASSES),
                in_=wb_words.rearrange("a p c i -> p a (c i)").bitcast(I32),
            )
            for r in range(4):
                nc.sync.dma_start(
                    out=wbs[r:P:32, :].bitcast(I32).rearrange("q (a c) -> q a c", a=PASSES),
                    in_=wb_scales[:, r:16:4, :].rearrange("a q c -> q a c").bitcast(I32),
                )

        w1_first = w1[:, 0:PASS].rearrange("(p t) c -> p t c", t=PACK)
        nc.sync.dma_start(offs_t[:], offs)
        nc.sync.dma_start(pos1_t[:], pos1)
        nc.sync.dma_start(pos2_t[:], pos2)
        nc.sync.dma_start(out=gain_t[:], in_=gain.rearrange("(b p t) -> p b t", p=P, t=PACK))
        nc.sync.dma_start(out=b1_t[:], in_=b1.rearrange("(b p t) -> p b t", p=P, t=PACK))
        nc.sync.dma_start(out=w2w_raw[:].bitcast(I32), in_=w2_words[0].bitcast(I32))
        for u in range(2):
            nc.sync.dma_start(out=raw[0][:, u, :], in_=w1_first[:, u, :])
        load_scales(tabs, tab_scales[0])
        for u in range(2, PACK):
            nc.sync.dma_start(out=raw[0][:, u, :], in_=w1_first[:, u, :])
        load_scales(w2s_raw, w2_scales[0])
        nc.sync.dma_start(out=tabw[:].bitcast(I32), in_=tab_words[0].rearrange("p c i -> p (c i)").bitcast(I32))
        load_w1(1)
        load_w1(2)
        load_wa(0)
        load_reading(0)

        def quantise(q, grp, j0, w):
            nc.vector.quantize_mx(out=q[0][:, j0:j0 + w].bitcast(E4M3), scales=q[1][:, j0:j0 + w], in_=grp)

        def w1_views(b):
            dst = wgrp[b % 2][:].rearrange("p (t m j) -> p m j t", t=PACK, j=PACK)
            src = raw[b][:].rearrange("p j (m t) -> p m j t", t=PACK)
            return dst, src

        nc.vector.tensor_copy(
            w2w[:].bitcast(U16).rearrange("p (b t m) -> p b t m", t=PACK, m=P),
            w2w_raw[:].bitcast(U16).rearrange("p (b m t) -> p b t m", t=PACK, m=P),
        )
        for i in range(2):
            nc.vector.tensor_copy(vs[i][:], tabs[:].indirect(offs_t[:, 32 * i:32 * (i + 1)]))
        dst, src = w1_views(0)
        nc.scalar.copy(dst, src)
        quantise(w1q[0], wgrp[0][:], 0, PASS)

        nc.vector.tensor_copy(
            w2s[:].rearrange("p (b t m) -> p b t m", t=PACK, m=P),
            w2s_raw[:].rearrange("p (b m t) -> p b t m", t=PACK, m=P),
        )
        for i in range(2):
            nc.vector.tensor_copy(vw[i][:], tabw[:].indirect(offs_t[:, 32 * i:32 * (i + 1)]))

        def first_stage(s, i, turn):
            b, t = divmod(s, PACK)
            cols = slice(P * t, P * (t + 1))
            bank_a = banks[turn % 4]
            bank_b = banks[4 + turn % 4]
            half = h[s][:, BANK * i:BANK * (i + 1)]
            nc.tensor.matmul_mx(
                out=bank_a[:], lhsT=w1q[b][0][:, cols].bitcast(E4M3), lhsT_scale=w1q[b][1][:, cols],
                rhs=vw[i][:].bitcast(E4M3), rhs_scale=vs[i][:], start=True, stop=True,
            )
            nc.tensor.matmul_mx(
                out=bank_b[:], lhsT=w2w[:, 2 * P * s:2 * P * (s + 1)].bitcast(E2M1), lhsT_scale=w2s[:, P * s:P * (s + 1)],
                rhs=vw[i][:].bitcast(E4M3), rhs_scale=vs[i][:], start=True, stop=True,
            )
            nc.scalar.activation(half, bank_a[:], ACT.Tanh, bias=b1_t[:, b, t:t + 1])
            nc.vector.tensor_tensor(half, bank_b[:], half, ALU.add)
            nc.gpsimd.tensor_scalar(half, half, gain_t[:, b, t:t + 1], 0.0, ALU.mult, ALU.add)

        def pick_b(dst, s, j0, w):
            nc.vector.tensor_copy(dst[:, s % PACK, :], h[s][:].indirect(pos2_t[:, j0 // 16:(j0 + w) // 16]))

        def pick_a(dst, s, j0, w):
            nc.vector.tensor_tensor(
                dst[:, s % PACK, :], h[s][:].indirect(pos1_t[:, j0 // 16:(j0 + w) // 16]),
                rd[s // PACK][:, s % PACK, j0:j0 + w], ALU.mult,
            )

        def pick_early(s):
            pick_b(early[s // PACK], s, 0, J)

        def prepare_w1(b):
            dst, src = w1_views(b)
            for m0 in range(0, P, P // 1):
                nc.scalar.copy(dst[:, m0:m0 + P // 1], src[:, m0:m0 + P // 1])
            quantise(w1q[b], wgrp[b % 2][:], 0, PASS)

        def weave(grp, src, func, q, j0, w):
            dst = grp.rearrange("p (c i t) -> p c t i", i=4, t=PACK)
            picked = src.rearrange("p t (c i) -> p c t i", i=4)
            step = min(w, 512) // 4
            for c0 in range(0, w // 4, step):
                nc.scalar.activation(dst[:, c0:c0 + step], picked[:, c0:c0 + step], func)
            quantise(q, grp, j0, w)

        def prepare_wa(b):
            weave(wa_woven[b], raw[(b + 3) % 4][:], ACT.Copy, waq[b], 0, N)

        def prepare_early(b):
            weave(early_woven[b], early[b], ACT.Abs, xbq[b], 0, J)

        def scores_late(piece, b):
            j0, w, first_bank = PIECES[piece]
            per_bank = BANK // w
            jc = slice(j0, j0 + w)
            for nt in range(4):
                place = nt % per_bank
                wc = slice(P * nt, P * (nt + 1))
                nc.tensor.matmul_mx(
                    out=banks[first_bank + nt // per_bank][:, w * place:w * (place + 1)],
                    lhsT=waq[b][0][:, wc].bitcast(E4M3), lhsT_scale=waq[b][1][:, wc],
                    rhs=xaq[b][0][:, jc].bitcast(E4M3), rhs_scale=xaq[b][1][:, jc],
                    start=(b == 0 and place == 0), stop=(b == PASSES - 1 and place == per_bank - 1),
                )

        def finish(piece):
            j0, w, first_bank = PIECES[piece]
            per_bank = BANK // w
            for k in range(4 // per_bank):
                bank = first_bank + k
                result = piece_result[bank].rearrange("p (u c) -> p u c", c=w)
                nc.vector.tensor_tensor(
                    result, banks[bank][:].rearrange("p (u c) -> p u c", c=w),
                    raw[2][:, per_bank * k:per_bank * (k + 1), j0:j0 + w], ALU.mult,
                )
                rows = out[P * per_bank * k:P * per_bank * (k + 1), j0:j0 + w]
                nc.sync.dma_start(out=rows.rearrange("(u p) c -> p u c", p=P), in_=result)

        def slices(first, end):
            for s in range(first, end):
                for i in range(2):
                    first_stage(s, i, 2 * s + i)
                pick_early(s - 1)

        for turn, (s, i) in enumerate(((0, 0), (1, 0), (0, 1), (1, 1))):
            first_stage(s, i, turn)
        pick_early(0)
        slices(2, 4)
        prepare_w1(1)
        load_wa(1)
        load_reading(1)
        load_wa(2)
        load_reading(2)
        load_wb()
        slices(4, 8)
        prepare_w1(2)
        slices(8, 12)
        pick_early(11)
        prepare_early(0)
        prepare_early(1)
        prepare_early(2)
        prepare_wa(0)
        prepare_wa(2)
        prepare_wa(1)
        for b in range(PASSES):
            for nt in range(4):
                wc = slice(P * nt, P * (nt + 1))
                nc.tensor.matmul_mx(
                    out=banks[nt][:], lhsT=wbq[b][0][:, wc].bitcast(E4M3), lhsT_scale=wbq[b][1][:, wc],
                    rhs=xbq[b][0][:].bitcast(E4M3), rhs_scale=xbq[b][1][:], start=(b == 0), stop=(b == PASSES - 1),
                )
        last = PASSES - 1
        for b in range(last):
            for t in range(PACK):
                pick_a(late[b], PACK * b + t, 0, J)
            weave(late_woven[b], late[b], ACT.Copy, xaq[b], 0, J)
            if b == 0:
                for nt in range(4):
                    nc.scalar.copy(raw[2][:, nt, :], banks[nt][:])
            if b == 0:
                for piece in range(len(PIECES)):
                    scores_late(piece, b)
        for piece, (j0, w, first_bank) in enumerate(PIECES):
            for t in range(PACK):
                pick_a(piece_picked[piece], PACK * last + t, j0, w)
            weave(piece_woven[piece], piece_picked[piece], ACT.Copy, xaq[last], j0, w)
            for b in range(1, PASSES):
                scores_late(piece, b)
        for piece in range(len(PIECES)):
            finish(piece)
